import numpy as np, ml_dtypes
CORES = [0,11,22,25,36,47,50,61,64,75,86,89]
N = 12
TOK = 64
ROUTE = [[[5,6],[3,5],[2,10],[2,8],[9,11],[6,11],[2,3],[1,4],[6,8],[4,9],[8,11],[3,4],[0,4],[0,8],[5,9],[0,9],[6,10],[3,11],[1,3],[0,1],[10,11],[4,10],[2,6],[1,8],[7,9],[3,9],[5,11],[2,7],[0,2],[0,7],[4,11],[5,8],[4,11],[4,8],[2,4],[6,7],[7,10],[5,9],[1,6],[5,8],[6,9],[8,9],[3,9],[4,6],[0,5],[6,9],[3,5],[0,4],[0,7],[6,7],[7,9],[9,10],[1,5],[0,6],[2,10],[1,5],[0,11],[9,11],[8,9],[5,7],[10,11],[0,5],[6,7],[5,6]],[[1,4],[9,11],[7,8],[9,10],[0,9],[1,8],[3,4],[6,8],[0,11],[1,9],[0,10],[6,11],[6,7],[0,10],[3,10],[3,4],[3,10],[1,6],[4,5],[0,3],[7,8],[2,9],[6,7],[2,5],[0,1],[2,11],[3,8],[1,5],[8,10],[7,11],[6,9],[2,6],[4,10],[1,3],[2,8],[7,8],[1,8],[2,6],[4,11],[6,8],[3,6],[2,7],[0,9],[6,10],[3,5],[0,6],[0,6],[2,6],[5,7],[7,9],[1,7],[9,10],[3,6],[5,11],[0,5],[4,10],[0,3],[1,6],[1,2],[0,1],[1,7],[0,1],[3,5],[9,10]],[[1,3],[1,4],[7,8],[1,6],[6,11],[2,11],[2,3],[2,11],[1,9],[0,10],[5,6],[1,9],[9,11],[1,11],[3,6],[7,8],[1,7],[1,9],[0,4],[4,10],[1,3],[4,8],[4,7],[1,3],[0,10],[10,11],[1,9],[0,10],[3,11],[5,11],[3,8],[5,6],[8,9],[5,9],[3,5],[0,6],[1,7],[2,5],[0,4],[6,9],[1,6],[4,6],[0,4],[1,6],[2,8],[6,7],[8,11],[0,4],[1,3],[2,6],[2,6],[8,10],[8,11],[8,10],[1,4],[7,11],[3,6],[4,5],[5,10],[4,9],[2,3],[2,9],[3,4],[1,9]],[[2,11],[4,9],[7,8],[2,7],[6,10],[1,11],[5,11],[0,11],[6,9],[0,9],[9,11],[2,8],[5,11],[6,7],[0,11],[4,7],[2,5],[8,10],[10,11],[6,11],[8,11],[5,6],[3,10],[9,10],[1,9],[7,8],[1,7],[1,3],[2,7],[0,7],[4,10],[5,10],[6,7],[0,4],[8,11],[4,6],[0,2],[0,2],[7,11],[0,2],[3,4],[9,10],[0,8],[2,10],[4,8],[6,8],[1,7],[0,10],[1,4],[6,8],[0,3],[0,7],[10,11],[1,5],[3,8],[3,6],[4,11],[7,10],[4,10],[3,5],[0,8],[2,11],[4,8],[3,11]],[[8,10],[3,4],[4,6],[5,8],[5,7],[6,9],[0,8],[5,9],[1,4],[1,2],[8,11],[3,6],[5,6],[5,11],[6,11],[7,11],[7,11],[8,10],[5,11],[1,3],[0,6],[7,11],[3,8],[5,6],[8,11],[7,8],[6,8],[0,11],[3,8],[2,6],[4,11],[0,3],[3,10],[1,4],[2,7],[2,11],[3,4],[1,10],[3,11],[6,10],[10,11],[0,11],[4,11],[6,9],[8,11],[6,8],[6,8],[3,5],[1,4],[5,11],[0,1],[2,7],[3,7],[4,11],[3,6],[4,11],[0,3],[1,9],[1,3],[1,7],[0,11],[0,9],[8,11],[5,11]],[[10,11],[6,8],[0,9],[0,6],[5,7],[1,10],[5,9],[2,4],[1,10],[8,11],[1,11],[2,3],[7,10],[5,10],[6,9],[5,6],[5,10],[8,10],[2,6],[5,6],[1,8],[0,11],[3,5],[1,2],[3,4],[5,9],[4,9],[0,8],[8,10],[5,7],[0,1],[3,6],[8,10],[3,4],[4,7],[0,2],[5,7],[6,7],[2,5],[8,10],[3,10],[5,6],[4,6],[1,6],[1,7],[7,10],[3,9],[1,8],[1,4],[0,3],[2,8],[3,10],[6,8],[6,8],[5,9],[1,11],[3,11],[4,8],[0,10],[6,10],[0,3],[1,4],[9,11],[3,10]],[[10,11],[1,10],[2,7],[6,11],[3,6],[1,5],[3,10],[2,3],[0,11],[4,11],[2,11],[5,11],[2,5],[2,5],[2,10],[7,10],[3,11],[5,8],[4,7],[7,11],[3,7],[6,10],[0,6],[8,11],[1,8],[5,11],[6,7],[2,8],[1,6],[0,8],[5,8],[3,7],[5,6],[2,6],[0,5],[4,5],[3,7],[1,6],[5,9],[3,9],[6,9],[3,7],[6,7],[4,11],[2,11],[7,11],[4,9],[1,4],[3,7],[1,7],[7,11],[0,9],[2,3],[3,11],[0,8],[7,9],[4,8],[7,10],[6,10],[7,11],[0,1],[3,11],[2,11],[3,8]],[[0,2],[3,7],[8,10],[1,3],[0,1],[0,5],[6,8],[8,11],[3,4],[2,11],[3,11],[1,4],[2,5],[7,9],[7,8],[4,7],[1,10],[7,8],[6,11],[2,11],[5,9],[7,9],[4,6],[10,11],[4,7],[5,9],[8,9],[5,11],[1,10],[2,7],[4,7],[2,3],[4,7],[2,5],[0,3],[1,2],[1,10],[7,10],[4,10],[2,5],[5,7],[6,10],[1,6],[1,9],[8,9],[2,10],[7,9],[8,10],[2,10],[3,4],[3,7],[0,8],[2,5],[1,4],[7,10],[5,9],[3,6],[8,10],[0,6],[7,10],[3,4],[1,8],[2,11],[3,4]],[[6,11],[4,11],[6,10],[3,9],[0,3],[2,8],[5,10],[6,9],[3,4],[10,11],[10,11],[7,11],[0,6],[0,3],[3,4],[1,7],[1,11],[3,4],[5,8],[2,10],[2,11],[1,5],[3,4],[3,6],[0,11],[2,9],[3,9],[2,10],[3,10],[3,8],[1,5],[2,6],[0,7],[1,10],[4,8],[1,7],[1,5],[7,11],[1,9],[3,10],[7,9],[5,10],[3,8],[0,8],[1,2],[2,11],[0,10],[0,1],[1,2],[2,11],[1,6],[4,5],[4,10],[2,10],[6,10],[1,11],[1,9],[1,4],[1,6],[5,9],[4,6],[0,3],[8,11],[6,7]],[[5,11],[4,9],[3,5],[0,7],[3,5],[4,8],[1,6],[0,10],[1,10],[5,7],[6,11],[7,8],[5,9],[0,3],[2,11],[1,5],[6,7],[1,7],[7,9],[0,10],[1,5],[3,4],[4,10],[1,4],[5,9],[4,8],[7,8],[7,10],[7,8],[4,11],[2,6],[3,10],[10,11],[1,11],[1,6],[1,7],[8,9],[6,10],[1,7],[2,6],[3,9],[3,9],[9,10],[3,8],[0,4],[6,10],[1,10],[8,11],[3,5],[6,9],[7,11],[0,9],[0,10],[5,6],[3,4],[8,9],[3,11],[2,4],[1,3],[5,9],[7,9],[3,5],[1,3],[8,9]],[[1,5],[1,8],[1,9],[1,9],[3,4],[1,9],[5,8],[0,10],[1,4],[3,6],[2,7],[0,11],[0,7],[4,8],[0,10],[0,5],[0,8],[1,2],[1,10],[6,11],[2,9],[7,11],[1,10],[10,11],[2,7],[5,7],[2,3],[0,10],[8,10],[5,10],[4,7],[5,10],[0,6],[4,5],[2,4],[7,8],[2,9],[3,7],[3,11],[0,9],[5,8],[0,7],[0,4],[1,5],[2,9],[1,11],[1,9],[0,3],[1,4],[2,6],[4,7],[4,10],[7,11],[3,6],[0,8],[6,9],[10,11],[0,2],[4,9],[7,8],[4,7],[6,10],[0,2],[4,7]],[[6,8],[2,7],[1,6],[0,10],[5,7],[3,9],[3,6],[0,4],[3,5],[6,8],[0,8],[3,4],[7,9],[7,10],[2,10],[4,7],[6,10],[1,11],[4,6],[2,4],[1,9],[4,7],[3,7],[1,11],[0,8],[7,9],[1,9],[1,3],[1,3],[5,8],[5,9],[3,4],[0,6],[3,5],[0,3],[1,5],[5,6],[0,9],[2,5],[0,3],[9,11],[2,8],[1,10],[1,7],[2,8],[3,8],[4,9],[9,11],[4,9],[1,3],[2,7],[3,4],[3,6],[3,4],[6,7],[3,9],[1,10],[2,8],[6,11],[6,7],[2,4],[6,11],[7,11],[3,7]]]
def setup_inputs(rng):
    return {"x": rng.standard_normal((N, 128, TOK), dtype=np.float32).astype(ml_dtypes.bfloat16), "w": rng.standard_normal((N, 128, 128), dtype=np.float32).astype(ml_dtypes.bfloat16)}
def reference(x, w):
    X, W = x.astype(np.float64), w.astype(np.float64)
    y = np.zeros((N, 128, TOK))
    for r in range(N):
        for t in range(TOK):
            for e in ROUTE[r][t]:
                y[r][:, t] += W[e].T @ X[r][:, t]
    return {"y": y.astype(ml_dtypes.bfloat16 if x.dtype != np.float64 else np.float64)}

@@ -1,0 +1,171 @@
+from concourse.bass import DstId, RemoteDMATransfer
+from concourse.mybir import dt, AluOpType
+
+NR = 12
+D = 128
+TK = 64
+
+SCRATCH = {
+    "wd": ("dram", [NR, D, D], "bfloat16"),
+    "wall": ("sbuf", [D, NR * D], "bfloat16"),
+    "xs": ("sbuf", [D, TK], "bfloat16"),
+    "mask": ("sbuf", [D, NR * TK], "bfloat16"),
+    "xm": ("sbuf", [D, NR * TK], "bfloat16"),
+    "ysb": ("sbuf", [D, TK], "bfloat16"),
+    "ps": ("psum", [D, TK], "float32"),
+}
+SEMAPHORES = ["arr%d" % e for e in range(NR)] + ["ldw", "ldx", "ldo", "vs", "xr", "mm", "cp", "st", "sent"]
+
+
+def _bits(m):
+    return bin(m).count("1")
+
+
+def _plan(T, topo):
+    cores = list(T.cores)
+    home = {}
+    for r, c in enumerate(cores):
+        home[topo.chip(c)] = r
+    chips = sorted(home)
+    sim = range((max(chips) + 1) * topo.CORES_PER_CHIP)
+    mate = {a: [b for b in chips if topo.mates(a, b)][0] for a in chips}
+    ring = {a: sorted([a] + [b for b in chips if topo.same_plane(a, b)]) for a in chips}
+    helpers, owns_port = {}, {}
+    for a in chips:
+        rc, far = cores[home[a]], cores[home[mate[a]]]
+        owns_port[a] = topo.may_write(rc, far)
+        bydie = {}
+        for c in sim:
+            if topo.chip(c) == a and c != rc and topo.may_write(c, far):
+                bydie.setdefault(topo.die(c), []).append(c)
+        groups = sorted(bydie.values(), key=lambda q: -len(q))
+        helpers[a] = [q[i] for i in range(len(groups[0])) for q in groups if i < len(q)]
+    calls, when = {}, {r: {r: -1.0} for r in range(len(cores))}
+    for a in chips:
+        r, n, i = home[a], len(ring[a]), ring[a].index(a)
+        first = []
+        for s in range(1, n):
+            b = ring[a][(i + s) % n]
+            h = helpers[b]
+            f = h[(s - 1 + (0 if owns_port[b] else 1)) % len(h)]
+            first.append(f)
+            calls.setdefault(f, []).append((s, r, [cores[home[b]], cores[home[mate[b]]]]))
+            when[home[b]][r] = s
+            when[home[mate[b]]][r] = s + 0.5
+        if owns_port[a]:
+            first.append(cores[home[mate[a]]])
+            when[home[mate[a]]][r] = 2.7
+        else:
+            f = helpers[a][0]
+            first.append(f)
+            calls.setdefault(f, []).append((0, r, [cores[home[mate[a]]]]))
+            when[home[mate[a]]][r] = 0.5
+        calls[cores[r]] = [(0, r, first)]
+    for c in calls:
+        calls[c].sort()
+    order = {r: sorted(when[r], key=lambda e: when[r][e]) for r in when}
+    return calls, order
+
+
+def _runs(cols, length):
+    left, out = set(cols), []
+    while left:
+        best = (0, 0, 1)
+        for a in sorted(left):
+            for d in range(1, length - a + 1):
+                n = 1
+                while a + n * d in left:
+                    n += 1
+                if n > best[0]:
+                    best = (n, a, d)
+        n, a, d = best
+        out.append((a, d, n))
+        for k in range(n):
+            left.discard(a + k * d)
+    return out
+
+
+def rank_program(g, core, T, topo):
+    calls, order = _plan(T, topo)
+    sem = T.sem
+    rank = T.rank_of(core)
+
+    def slot(e):
+        return T.wall[:, e * D:(e + 1) * D]
+
+    def engines(src, dst):
+        m = topo.mask(src, dst)
+        if topo.chip(src) == topo.chip(dst):
+            away = [c for c in T.cores if topo.chip(c) != topo.chip(src)][0]
+            m &= ~topo.mask(src, away)
+        return m
+
+    def landed(e):
+        for src in calls:
+            for _, ee, dests in calls[src]:
+                if ee == e and core in dests:
+                    return _bits(engines(src, core))
+
+    def send(e, dests):
+        trs, n = [], 0
+        for group in ([c for c in dests if topo.chip(c) != topo.chip(core)],
+                      [c for c in dests if topo.chip(c) == topo.chip(core)]):
+            if group:
+                ids = []
+                for c in group:
+                    rid, pid, _ = topo.addr(c)
+                    ids.append(DstId(rid=rid, pnc=pid))
+                m = engines(core, group[0])
+                trs.append(RemoteDMATransfer(dst_ids=ids, dma_engine_mask=m, remote_sem=sem["arr%d" % e],
+                                             srcs=[T.wd[e]],
+                                             dsts=[T.wd[e] if T.rank_of(c) is None else slot(e) for c in group],
+                                             alu_op=0))
+                n += _bits(m)
+        g.remote_dma_fused(trs, local_sem=sem.sent)
+        return n
+
+    if rank is not None:
+        g.sync.dma_start(T.wd[rank], T.w[:]).then_inc(sem.ldw, 16)
+        g.scalar.dma_start(T.xs[:], T.x[:]).then_inc(sem.ldx, 16)
+        g.scalar.dma_start(slot(rank), T.w[:]).then_inc(sem.ldo, 16)
+
+    sent = 0
+    for _, e, dests in calls.get(core, []):
+        if e == rank:
+            g.wait_ge(sem.ldw, 16)
+        else:
+            g.wait_ge(sem["arr%d" % e], landed(e))
+        sent += send(e, dests)
+    if sent:
+        g.wait_ge(sem.sent, sent)
+    if rank is None:
+        return
+
+    route = T.tables["ROUTE"][rank]
+    v = g.vector
+    v.memset(T.mask[:], 0.0).then_inc(sem.vs, 1)
+    v.wait_ge(sem.vs, 1)
+    fills = _runs([e * TK + t for t in range(TK) for e in route[t]], NR * TK)
+    for a, d, n in fills:
+        v.memset(T.mask[:, a:a + (n - 1) * d + 1:d], 1.0).then_inc(sem.vs, 1)
+    v.wait_ge(sem.vs, 1 + len(fills))
+    v.wait_ge(sem.ldx, 16)
+    for e in order[rank]:
+        v.tensor_tensor(T.xm[:, e * TK:(e + 1) * TK], T.xs[:], T.mask[:, e * TK:(e + 1) * TK],
+                        AluOpType.mult).then_inc(sem.xr, 1)
+
+    te = g.tensor
+    te.wait_ge(sem.xr, NR)
+    for k, e in enumerate(order[rank]):
+        if e == rank:
+            te.wait_ge(sem.ldo, 16)
+        else:
+            te.wait_ge(sem["arr%d" % e], landed(e))
+        mm = te.matmul(T.ps[:], slot(e), T.xm[:, e * TK:(e + 1) * TK], start=(k == 0), stop=(k == NR - 1))
+    mm.then_inc(sem.mm, 1)
+
+    v.wait_ge(sem.mm, 1)
+    v.tensor_copy(T.ysb[:], T.ps[:]).then_inc(sem.cp, 1)
+    g.sync.wait_ge(sem.cp, 1)
+    g.sync.dma_start(T.y[:], T.ysb[:]).then_inc(sem.st, 16)
+    g.sync.wait_ge(sem.st, 16)

@@ -4,6 +4,7 @@ from concourse.mybir import dt, AluOpType
 NR = 12
 D = 128
 TK = 64
+XF = 3
 
 SCRATCH = {
     "wd": ("dram", [NR, D, D], "bfloat16"),
@@ -30,7 +31,7 @@ def _plan(T, topo):
     sim = range((max(chips) + 1) * topo.CORES_PER_CHIP)
     mate = {a: [b for b in chips if topo.mates(a, b)][0] for a in chips}
     ring = {a: sorted([a] + [b for b in chips if topo.same_plane(a, b)]) for a in chips}
-    helpers, owns_port = {}, {}
+    ports, idle, owns_port = {}, {}, {}
     for a in chips:
         rc, far = cores[home[a]], cores[home[mate[a]]]
         owns_port[a] = topo.may_write(rc, far)
@@ -39,28 +40,38 @@ def _plan(T, topo):
             if topo.chip(c) == a and c != rc and topo.may_write(c, far):
                 bydie.setdefault(topo.die(c), []).append(c)
         groups = sorted(bydie.values(), key=lambda q: -len(q))
-        helpers[a] = [q[i] for i in range(len(groups[0])) for q in groups if i < len(q)]
+        ports[a] = [q[i] for i in range(len(groups[0])) for q in groups if i < len(q)]
+        rest = [c for c in sim if topo.chip(c) == a and c != rc and not topo.may_write(c, far)]
+        idle[a] = sorted(rest, key=lambda c: topo.die(c) == topo.die(rc))
+    n = len(ring[chips[0]])
+    nown = 1 + (n - 1 - XF)
+    take = {a: ((2 if nown >= 3 else 1) if owns_port[a] else 0) for a in chips}
     calls, when = {}, {r: {r: -1.0} for r in range(len(cores))}
     for a in chips:
-        r, n, i = home[a], len(ring[a]), ring[a].index(a)
-        first = []
-        for s in range(1, n):
-            b = ring[a][(i + s) % n]
-            h = helpers[b]
-            f = h[(s - 1 + (0 if owns_port[b] else 1)) % len(h)]
-            first.append(f)
+        r, i = home[a], ring[a].index(a)
+        peers = [ring[a][(i + s) % n] for s in range(1, n)]
+        away, near = [], []
+        for s, b in enumerate(peers[:XF], 1):
+            f = ports[b][(nown - take[b] + s - 1) % len(ports[b])]
+            away.append(f)
             calls.setdefault(f, []).append((s, r, [cores[home[b]], cores[home[mate[b]]]]))
-            when[home[b]][r] = s
-            when[home[mate[b]]][r] = s + 0.5
-        if owns_port[a]:
-            first.append(cores[home[mate[a]]])
-            when[home[mate[a]]][r] = 2.7
-        else:
-            f = helpers[a][0]
-            first.append(f)
-            calls.setdefault(f, []).append((0, r, [cores[home[mate[a]]]]))
-            when[home[mate[a]]][r] = 0.5
-        calls[cores[r]] = [(0, r, first)]
+            when[home[b]][r] = s + 4.0
+            when[home[mate[b]]][r] = s + 4.2
+        own = [mate[a]] + [mate[b] for b in peers[XF:]]
+        for k, b in enumerate(own[:take[a]]):
+            away.append(cores[home[b]])
+            when[home[b]][r] = XF + 1.5 * (k + 1)
+        for k, b in enumerate(own[take[a]:]):
+            f = ports[a][k % len(ports[a])]
+            near.append(f)
+            calls.setdefault(f, []).append((0, r, [cores[home[b]]]))
+            when[home[b]][r] = 4.0 + 0.5 * k
+        for k, b in enumerate(peers[XF:]):
+            f = idle[a][k % len(idle[a])]
+            near.append(f)
+            calls.setdefault(f, []).append((0, r, [cores[home[b]]]))
+            when[home[b]][r] = 4.1 + 0.5 * (k + nown - take[a])
+        calls[cores[r]] = [(0, r, away + near)]
     for c in calls:
         calls[c].sort()
     order = {r: sorted(when[r], key=lambda e: when[r][e]) for r in when}

from concourse.bass import DstId, RemoteDMATransfer
from concourse.mybir import dt, AluOpType

NR = 12
D = 128
TK = 64
XF = 3

SCRATCH = {
    "wd": ("dram", [NR, D, D], "bfloat16"),
    "wall": ("sbuf", [D, NR * D], "bfloat16"),
    "xs": ("sbuf", [D, TK], "bfloat16"),
    "mask": ("sbuf", [D, NR * TK], "bfloat16"),
    "xm": ("sbuf", [D, NR * TK], "bfloat16"),
    "ysb": ("sbuf", [D, TK], "bfloat16"),
    "ps": ("psum", [D, TK], "float32"),
}
SEMAPHORES = ["arr%d" % e for e in range(NR)] + ["ldw", "ldx", "ldo", "vs", "xr", "mm", "cp", "st", "sent"]


def _bits(m):
    return bin(m).count("1")


def _plan(T, topo):
    cores = list(T.cores)
    home = {}
    for r, c in enumerate(cores):
        home[topo.chip(c)] = r
    chips = sorted(home)
    sim = range((max(chips) + 1) * topo.CORES_PER_CHIP)
    mate = {a: [b for b in chips if topo.mates(a, b)][0] for a in chips}
    ring = {a: sorted([a] + [b for b in chips if topo.same_plane(a, b)]) for a in chips}
    ports, idle, owns_port = {}, {}, {}
    for a in chips:
        rc, far = cores[home[a]], cores[home[mate[a]]]
        owns_port[a] = topo.may_write(rc, far)
        bydie = {}
        for c in sim:
            if topo.chip(c) == a and c != rc and topo.may_write(c, far):
                bydie.setdefault(topo.die(c), []).append(c)
        groups = sorted(bydie.values(), key=lambda q: -len(q))
        ports[a] = [q[i] for i in range(len(groups[0])) for q in groups if i < len(q)]
        rest = [c for c in sim if topo.chip(c) == a and c != rc and not topo.may_write(c, far)]
        idle[a] = sorted(rest, key=lambda c: topo.die(c) == topo.die(rc))
    n = len(ring[chips[0]])
    nown = 1 + (n - 1 - XF)
    take = {a: ((2 if nown >= 3 else 1) if owns_port[a] else 0) for a in chips}
    calls, when = {}, {r: {r: -1.0} for r in range(len(cores))}
    for a in chips:
        r, i = home[a], ring[a].index(a)
        peers = [ring[a][(i + s) % n] for s in range(1, n)]
        away, near = [], []
        for s, b in enumerate(peers[:XF], 1):
            f = ports[b][(nown - take[b] + s - 1) % len(ports[b])]
            away.append(f)
            calls.setdefault(f, []).append((s, r, [cores[home[b]], cores[home[mate[b]]]]))
            when[home[b]][r] = s + 4.0
            when[home[mate[b]]][r] = s + 4.2
        own = [mate[a]] + [mate[b] for b in peers[XF:]]
        for k, b in enumerate(own[:take[a]]):
            away.append(cores[home[b]])
            when[home[b]][r] = XF + 1.5 * (k + 1)
        for k, b in enumerate(own[take[a]:]):
            f = ports[a][k % len(ports[a])]
            near.append(f)
            calls.setdefault(f, []).append((0, r, [cores[home[b]]]))
            when[home[b]][r] = 4.0 + 0.5 * k
        for k, b in enumerate(peers[XF:]):
            f = idle[a][k % len(idle[a])]
            near.append(f)
            calls.setdefault(f, []).append((0, r, [cores[home[b]]]))
            when[home[b]][r] = 4.1 + 0.5 * (k + nown - take[a])
        calls[cores[r]] = [(0, r, away + near)]
    for c in calls:
        calls[c].sort()
    order = {r: sorted(when[r], key=lambda e: when[r][e]) for r in when}
    return calls, order


def _runs(cols, length):
    left, out = set(cols), []
    while left:
        best = (0, 0, 1)
        for a in sorted(left):
            for d in range(1, length - a + 1):
                n = 1
                while a + n * d in left:
                    n += 1
                if n > best[0]:
                    best = (n, a, d)
        n, a, d = best
        out.append((a, d, n))
        for k in range(n):
            left.discard(a + k * d)
    return out


def rank_program(g, core, T, topo):
    calls, order = _plan(T, topo)
    sem = T.sem
    rank = T.rank_of(core)

    def slot(e):
        return T.wall[:, e * D:(e + 1) * D]

    def engines(src, dst):
        m = topo.mask(src, dst)
        if topo.chip(src) == topo.chip(dst):
            away = [c for c in T.cores if topo.chip(c) != topo.chip(src)][0]
            m &= ~topo.mask(src, away)
        return m

    def landed(e):
        for src in calls:
            for _, ee, dests in calls[src]:
                if ee == e and core in dests:
                    return _bits(engines(src, core))

    def send(e, dests):
        trs, n = [], 0
        for group in ([c for c in dests if topo.chip(c) != topo.chip(core)],
                      [c for c in dests if topo.chip(c) == topo.chip(core)]):
            if group:
                ids = []
                for c in group:
                    rid, pid, _ = topo.addr(c)
                    ids.append(DstId(rid=rid, pnc=pid))
                m = engines(core, group[0])
                trs.append(RemoteDMATransfer(dst_ids=ids, dma_engine_mask=m, remote_sem=sem["arr%d" % e],
                                             srcs=[T.wd[e]],
                                             dsts=[T.wd[e] if T.rank_of(c) is None else slot(e) for c in group],
                                             alu_op=0))
                n += _bits(m)
        g.remote_dma_fused(trs, local_sem=sem.sent)
        return n

    if rank is not None:
        g.sync.dma_start(T.wd[rank], T.w[:]).then_inc(sem.ldw, 16)
        g.scalar.dma_start(T.xs[:], T.x[:]).then_inc(sem.ldx, 16)
        g.scalar.dma_start(slot(rank), T.w[:]).then_inc(sem.ldo, 16)

    sent = 0
    for _, e, dests in calls.get(core, []):
        if e == rank:
            g.wait_ge(sem.ldw, 16)
        else:
            g.wait_ge(sem["arr%d" % e], landed(e))
        sent += send(e, dests)
    if sent:
        g.wait_ge(sem.sent, sent)
    if rank is None:
        return

    route = T.tables["ROUTE"][rank]
    v = g.vector
    v.memset(T.mask[:], 0.0).then_inc(sem.vs, 1)
    v.wait_ge(sem.vs, 1)
    fills = _runs([e * TK + t for t in range(TK) for e in route[t]], NR * TK)
    for a, d, n in fills:
        v.memset(T.mask[:, a:a + (n - 1) * d + 1:d], 1.0).then_inc(sem.vs, 1)
    v.wait_ge(sem.vs, 1 + len(fills))
    v.wait_ge(sem.ldx, 16)
    for e in order[rank]:
        v.tensor_tensor(T.xm[:, e * TK:(e + 1) * TK], T.xs[:], T.mask[:, e * TK:(e + 1) * TK],
                        AluOpType.mult).then_inc(sem.xr, 1)

    te = g.tensor
    te.wait_ge(sem.xr, NR)
    for k, e in enumerate(order[rank]):
        if e == rank:
            te.wait_ge(sem.ldo, 16)
        else:
            te.wait_ge(sem["arr%d" % e], landed(e))
        mm = te.matmul(T.ps[:], slot(e), T.xm[:, e * TK:(e + 1) * TK], start=(k == 0), stop=(k == NR - 1))
    mm.then_inc(sem.mm, 1)

    v.wait_ge(sem.mm, 1)
    v.tensor_copy(T.ysb[:], T.ps[:]).then_inc(sem.cp, 1)
    g.sync.wait_ge(sem.cp, 1)
    g.sync.dma_start(T.y[:], T.ysb[:]).then_inc(sem.st, 16)
    g.sync.wait_ge(sem.st, 16)
